import numpy as np
import ml_dtypes


def mxq(x, axis, fmt="e4m3"):
    dtype, down = {"e4m3": (ml_dtypes.float8_e4m3fn, 7), "e5m2": (ml_dtypes.float8_e5m2, 14)}[fmt]
    v = np.moveaxis(np.asarray(x, np.float32).astype(ml_dtypes.bfloat16).astype(np.float64), axis, -1)
    blocks = v.reshape(v.shape[:-1] + (-1, 32))
    amax = np.abs(blocks).max(-1, keepdims=True)
    byte = np.maximum(np.where(amax > 0, np.frexp(amax)[1] - 1 + 127, 0) - down, 1)
    scale = np.exp2(byte - 127.0)
    codes = (blocks / scale).astype(np.float32).astype(dtype).astype(np.float64)
    return np.moveaxis((codes * scale).reshape(v.shape), -1, axis)


WIDE = False


def mx_kscale(k):
    if not WIDE:
        return np.ones(k)
    levels = np.array([10, -10, 5, -5, 0])
    if k % 512:
        return np.exp2(np.random.permutation(np.resize(levels, k // 32))).repeat(32)
    a = np.empty((k // 512, 16))
    for p in range(k // 512):
        a[p, :8] = np.random.permutation(np.resize(levels, 8))
        for g in range(8):
            far = levels[np.abs(levels - a[p, g]) >= 10]
            a[p, g + 8] = far[np.random.randint(len(far))]
    return np.exp2(a.ravel()).repeat(32)


def f64(x):
    return np.asarray(x).astype(np.float64)


def striped(idx):
    return np.tile(idx.reshape(-1, 16).T, (8, 1)).astype(np.uint16)


def unstriped(offs):
    return offs[:16].T.reshape(-1).astype(np.int64)


def striped8(idx):
    return np.concatenate([x.reshape(-1, 16).T for x in idx]).astype(np.uint16)


def runs(offs, k):
    lists = np.stack([offs[16 * r : 16 * r + 16].T.reshape(-1) for r in range(8)]).astype(np.int64)
    return lists[np.arange(k) % 512 // 64]


def pack_weight(w):
    k, n = w.shape
    w = f64(np.asarray(w, np.float32).astype(ml_dtypes.bfloat16)).reshape(k // 32, 32, n)
    amax = np.abs(w).max(1)
    byte = np.clip(np.where(amax > 0, np.frexp(amax)[1] - 1 + 127 - 7, 1), 1, 254)
    scaled = (w * np.exp2(127.0 - byte)[:, None, :]).reshape(k, n).astype(np.float32)
    words = np.ascontiguousarray(scaled.reshape(k // 512, 128, 4, n).transpose(0, 1, 3, 2)).astype(ml_dtypes.float8_e4m3fn).view(np.uint8)
    return words, np.ascontiguousarray(byte.astype(np.uint8).reshape(k // 512, 16, n))


def unpack_weight(words, scales):
    g, p, n, _ = words.shape
    vals = np.ascontiguousarray(words).view(ml_dtypes.float8_e4m3fn).astype(np.float64) * np.repeat(np.exp2(scales.astype(np.float64) - 127.0), 8, axis=1)[..., None]
    return vals.transpose(0, 1, 3, 2).reshape(g * 512, n)


K, T, S, N, H = 512, 2048, 512, 512, 512


def setup_inputs():
    n = np.random.standard_normal
    s = mx_kscale(K)[:, None]
    u = mx_kscale(S)
    packed_xT = pack_weight(n((K, T)) * s)
    return {
        "x_words": packed_xT[0],
        "x_scales": packed_xT[1],
        "wa": (n((K, H)) / np.sqrt(K) / s).astype(np.float32),
        "wb": (n((K, N)) / np.sqrt(K) / s).astype(np.float32),
        "gt": (np.random.uniform(0.5, 1.5, (S, 1)) * u[:, None]).astype(np.float32),
        "gi": (np.random.uniform(0.5, 1.5, (S, 1)) / u[:, None]).astype(np.float32),
        "offs": striped(np.random.permutation(T)[:S]),
        "two": striped(np.random.permutation(T)[:S]),
        "n1": striped8(np.stack([np.random.permutation(H) for _ in range(8)])),
        "n2": striped8(np.stack([np.random.permutation(H) for _ in range(8)])),
        "n3": striped8(np.stack([np.random.permutation(H) for _ in range(8)])),
        "n4": striped8(np.stack([np.random.permutation(N) for _ in range(8)])),
        "n5": striped8(np.stack([np.random.permutation(N) for _ in range(8)])),
    }


def reference(x_words, x_scales, wa, wb, gt, gi, offs, two, n1, n2, n3, n4, n5):
    xq = unpack_weight(x_words, x_scales)[:, unstriped(offs)]
    a = xq.T @ mxq(f64(wa), 0, "e4m3")
    b1 = a[np.arange(S)[:, None], runs(n1, S)]
    b2 = a[np.arange(S)[:, None], runs(n2, S)]
    b3 = a[np.arange(S)[:, None], runs(n3, S)]
    z = f64(gt) * (np.maximum(np.maximum(b1, b2), b3) - (0.5 * (np.maximum(np.minimum(b1, b2), np.minimum(np.maximum(b1, b2), b3)))))
    x_two = unpack_weight(x_words, x_scales)[:, unstriped(two)]
    b = x_two.T @ mxq(f64(wb), 0, "e4m3")
    z2 = f64(gi) * b
    cv = 0.0625 * ((mxq(z, 0, "e4m3").T @ mxq(z2, 0, "e4m3")))
    ex = np.exp(cv)
    return np.log(ex + ex[np.arange(H)[:, None], runs(n4, H)]) - (cv[np.arange(H)[:, None], runs(n5, H)])

@@ -1,0 +1,229 @@
+from contextlib import ExitStack
+
+import concourse.mybir as mybir
+from concourse.masks import make_identity
+
+K, T, S, H, N = 512, 2048, 512, 512, 512
+P = 128
+PACK = 4
+WIN = 1024
+
+F32 = mybir.dt.float32
+BF16 = mybir.dt.bfloat16
+I32 = mybir.dt.int32
+U32 = mybir.dt.uint32
+U16 = mybir.dt.uint16
+U8 = mybir.dt.uint8
+FP8X4 = mybir.dt.float8_e4m3fn_x4
+ALU = mybir.AluOpType
+ACT = mybir.ActivationFunctionType
+
+FLOPS = 2 * K * S * H + 2 * K * S * N + 2 * S * H * N
+
+
+def tile_picked_momtop2lse_none_p_kernel(
+    tc, x_words, x_scales, wa, wb, gt, gi, offs, two, n1, n2, n3, n4, n5, out
+):
+    nc = tc.nc
+    with ExitStack() as ctx:
+        lists = ctx.enter_context(tc.tile_pool(name="lists", bufs=1))
+        keep = ctx.enter_context(tc.tile_pool(name="keep", bufs=1))
+        work = ctx.enter_context(tc.tile_pool(name="work", bufs=2))
+        psum = ctx.enter_context(tc.psum_pool(name="psum", bufs=1))
+
+        def load_list(src, name):
+            tile = lists.tile([P, S // 16], U16, name=name)
+            nc.sync.dma_start(tile[:], src)
+            return tile
+
+        def bank(b):
+            return psum.tile([P, 512], F32, name="bank%d" % b)
+
+        x_sc = keep.tile([P, T], U8, align_bytes=64)
+        nc.vector.memset(x_sc[:].bitcast(I32), 0)
+        wa_raw = keep.tile([P, PACK, H], F32)
+        nc.sync.dma_start(wa_raw[:], wa.rearrange("(p j) c -> p j c", j=PACK))
+        for j in range(PACK):
+            nc.sync.dma_start(x_sc[j:P:32, :].bitcast(I32), x_scales[0, j:16:PACK, :].bitcast(I32))
+        offs_sb = load_list(offs, "offs_sb")
+        x_w = keep.tile([P, T], I32, align_bytes=64)
+        nc.sync.dma_start(x_w[:], x_words[0].rearrange("p n j -> p (n j)").bitcast(I32))
+        two_sb = load_list(two, "two_sb")
+        n1_sb = load_list(n1, "n1_sb")
+        n2_sb = load_list(n2, "n2_sb")
+        n3_sb = load_list(n3, "n3_sb")
+        wb_raw = keep.tile([P, PACK, N], F32)
+        nc.sync.dma_start(wb_raw[:], wb.rearrange("(p j) c -> p j c", j=PACK))
+        n4_sb = load_list(n4, "n4_sb")
+        n5_sb = load_list(n5, "n5_sb")
+
+        g_rows = keep.tile([P, P], F32)
+        nc.gpsimd.memset(g_rows[:], 0.0)
+        for row, g in ((0, gt), (PACK, gi)):
+            nc.gpsimd.dma_start(
+                g_rows[row : row + PACK, :].rearrange("t (q r) -> t q r", r=8),
+                g.rearrange("(q t r) o -> t q (r o)", t=PACK, r=8),
+            )
+        ident = keep.tile([P, P], F32)
+        make_identity(nc, ident[:])
+
+        a_win = [keep.tile([P, WIN], F32, name="a_win%d" % t) for t in range(PACK)]
+        ex_win = [keep.tile([P, WIN], F32, name="ex_win%d" % t) for t in range(PACK)]
+        for t in range(PACK):
+            nc.vector.memset(a_win[t][:, H:], 0.0)
+
+        g_cols = bank(7)
+        nc.tensor.transpose(g_cols[:, :P], g_rows[:], ident[:])
+        gt_half = keep.tile([P, PACK], F32)
+        nc.scalar.activation(gt_half[:], g_cols[:, 0:PACK], ACT.Abs, scale=0.5)
+        gt_sign = keep.tile([P, PACK], F32)
+        nc.scalar.activation(gt_sign[:], g_cols[:, 0:PACK], ACT.Sign)
+        gi_signed = keep.tile([P, PACK], F32)
+        nc.vector.tensor_tensor(gi_signed[:], g_cols[:, PACK : 2 * PACK], gt_sign[:], ALU.mult)
+
+        def pick_scales(offsets, name):
+            picked = keep.tile([P, S], U8, name=name + "_picked", align_bytes=64)
+            nc.vector.tensor_copy(picked[:], x_sc[:].indirect(offsets[:]))
+            dealt = keep.tile([P, S], U8, name=name, align_bytes=64)
+            nc.vector.tensor_copy(
+                dealt[:].bitcast(I32).rearrange("p (t q w) -> p q t w", t=PACK, w=2),
+                picked[:].bitcast(I32).rearrange("p (q t w) -> p q t w", t=PACK, w=2),
+            )
+            return dealt
+
+        def pick_words(offsets, name):
+            dealt = keep.tile([P, S], U32, name=name, align_bytes=64)
+            nc.vector.tensor_copy(
+                dealt[:].rearrange("p (t q r) -> p q t r", t=PACK, r=8),
+                x_w[:].bitcast(U32).indirect(offsets[:]),
+            )
+            return dealt
+
+        def interleave(copy, dst, src):
+            copy(
+                dst.rearrange("p (c i t) -> p c t i", i=4, t=PACK),
+                src.rearrange("p t (c i) -> p c t i", i=4),
+            )
+
+        def quantize(codes, scales, grouped):
+            nc.vector.quantize_mx(out=codes.bitcast(FP8X4), scales=scales, in_=grouped)
+
+        def product(acc, lhs, lhs_scales, rhs, rhs_scales):
+            nc.tensor.matmul_mx(
+                out=acc,
+                lhsT=lhs.bitcast(FP8X4),
+                lhsT_scale=lhs_scales,
+                rhs=rhs.bitcast(FP8X4),
+                rhs_scale=rhs_scales,
+                start=True,
+                stop=True,
+            )
+
+        xa_scales = pick_scales(offs_sb, "xa_scales")
+        xb_scales = pick_scales(two_sb, "xb_scales")
+
+        wa_codes = keep.tile([P, H], U32, align_bytes=64)
+        wa_scales = keep.tile([P, H], U8, align_bytes=64)
+        half = H // 2
+        for h, copy in ((0, nc.vector.tensor_copy), (1, nc.scalar.copy)):
+            grouped = keep.tile([P, half * PACK], BF16, name="wa_grouped%d" % h, align_bytes=64)
+            cols = slice(h * half, (h + 1) * half)
+            interleave(copy, grouped[:], wa_raw[:, :, cols])
+            quantize(wa_codes[:, cols], wa_scales[:, cols], grouped[:])
+
+        xa_words = pick_words(offs_sb, "xa_words")
+        xb_words = pick_words(two_sb, "xb_words")
+
+        for t in range(PACK):
+            cols = slice(t * P, (t + 1) * P)
+            acc = bank(t)
+            product(acc[:], xa_words[:, cols], xa_scales[:, cols], wa_codes[:], wa_scales[:])
+            nc.scalar.activation(a_win[t][:, :H], acc[:], ACT.Copy, scale=gt_half[:, t : t + 1])
+
+        wb_grouped = keep.tile([P, N * PACK], BF16, align_bytes=64)
+        interleave(nc.scalar.copy, wb_grouped[:], wb_raw[:])
+        wb_codes = keep.tile([P, N], U32, align_bytes=64)
+        wb_scales = keep.tile([P, N], U8, align_bytes=64)
+
+        z_rows = keep.tile([P, PACK, H], BF16, align_bytes=64)
+
+        def top2_steps(t):
+            def tmp(name):
+                return work.tile([P, H], F32, name=name)
+
+            b1, spread, hi, lead, bent = [tmp(name) for name in ("b1", "spread", "hi", "lead", "bent")]
+            d, e = ex_win[t][:, :H], ex_win[t][:, H:]
+            win = a_win[t]
+
+            def step_d():
+                nc.vector.tensor_tensor(d, win[:].indirect(n2_sb[:]), b1[:], ALU.subtract)
+                nc.scalar.activation(spread[:], d, ACT.Abs)
+
+            return [
+                lambda: nc.vector.tensor_copy(b1[:], win[:].indirect(n1_sb[:])),
+                step_d,
+                lambda: nc.vector.scalar_tensor_tensor(hi[:], d, 0.0, b1[:], ALU.max, ALU.add),
+                lambda: nc.vector.tensor_tensor(e, win[:].indirect(n3_sb[:]), hi[:], ALU.subtract),
+                lambda: nc.vector.scalar_tensor_tensor(lead[:], e, -1.0, spread[:], ALU.mult, ALU.min),
+                lambda: nc.vector.scalar_tensor_tensor(bent[:], lead[:], -2.0, lead[:], ALU.mult, ALU.max),
+                lambda: nc.vector.tensor_tensor(z_rows[:, t, :], bent[:], hi[:], ALU.add),
+            ]
+
+        def top2_pair(t):
+            for first, second in zip(top2_steps(t), top2_steps(t + 1)):
+                first()
+                second()
+
+        top2_pair(0)
+
+        quantize(wb_codes[:], wb_scales[:], wb_grouped[:])
+        z2_rows = keep.tile([P, PACK, N], BF16, align_bytes=64)
+        for t in range(PACK):
+            cols = slice(t * P, (t + 1) * P)
+            acc = bank(PACK + t)
+            product(acc[:], xb_words[:, cols], xb_scales[:, cols], wb_codes[:], wb_scales[:])
+            nc.scalar.activation(z2_rows[:, t, :], acc[:], ACT.Copy, scale=gi_signed[:, t : t + 1])
+        z2_grouped = keep.tile([P, N * PACK], BF16, align_bytes=64)
+        interleave(nc.scalar.copy, z2_grouped[:], z2_rows[:])
+
+        top2_pair(2)
+
+        z2_codes = keep.tile([P, N], U32, align_bytes=64)
+        z2_scales = keep.tile([P, N], U8, align_bytes=64)
+        quantize(z2_codes[:], z2_scales[:], z2_grouped[:])
+
+        z_by_block = z_rows[:].rearrange("p t (g u c i) -> p u g c t i", g=8, u=PACK, i=4)
+        z_grouped = [keep.tile([P, P * PACK], BF16, name="z_grouped%d" % u, align_bytes=64) for u in range(PACK)]
+        z_codes = keep.tile([P, H], U32, align_bytes=64)
+        z_scales = keep.tile([P, H], U8, align_bytes=64)
+
+        def group_z(u):
+            nc.vector.tensor_copy(
+                z_grouped[u][:].rearrange("p (g c i t) -> p g c t i", g=8, i=4, t=PACK), z_by_block[:, u]
+            )
+
+        ex = [keep.tile([P, N], F32, name="ex%d" % u) for u in range(PACK)]
+        cv_acc = []
+        group_z(0)
+        for u in range(PACK):
+            cols = slice(u * P, (u + 1) * P)
+            if u + 1 < PACK:
+                group_z(u + 1)
+            quantize(z_codes[:, cols], z_scales[:, cols], z_grouped[u][:])
+            acc = bank(u)
+            product(acc[:], z_codes[:, cols], z_scales[:, cols], z2_codes[:], z2_scales[:])
+            nc.scalar.activation(ex_win[u][:, :N], acc[:], ACT.Exp, scale=0.0625)
+            nc.scalar.activation(ex[u][:], acc[:], ACT.Exp, scale=0.0625)
+            cv_acc.append(acc)
+
+        pair_sum = [keep.tile([P, N], F32, name="pair_sum%d" % u) for u in range(PACK)]
+        for u in range(PACK):
+            nc.vector.tensor_tensor(pair_sum[u][:], ex_win[u][:].indirect(n4_sb[:]), ex[u][:], ALU.add)
+        out_rows = out.rearrange("(g u r) n -> u g r n", u=PACK, r=16)
+        for u in range(PACK):
+            nc.scalar.activation(a_win[u][:, :N], cv_acc[u][:], ACT.Copy, scale=-0.0625)
+            lse = work.tile([P, N], F32, name="lse")
+            nc.scalar.activation(lse[:], pair_sum[u][:], ACT.Ln)
+            res = keep.tile([P, N], F32, name="res%d" % u)
+            nc.vector.tensor_tensor(res[:], a_win[u][:].indirect(n5_sb[:]), lse[:], ALU.add)
+            nc.sync.dma_start(out_rows[u], res[:])

@@ -36,36 +36,42 @@ def tile_picked_momtop2lse_none_p_kernel(
             nc.sync.dma_start(tile[:], src)
             return tile
 
-        def bank(b):
-            return psum.tile([P, 512], F32, name="bank%d" % b)
+        def bank(b, dtype=F32):
+            return psum.tile([P, 512], dtype, name="bank%d" % b)
 
         x_sc = keep.tile([P, T], U8, align_bytes=64)
         nc.vector.memset(x_sc[:].bitcast(I32), 0)
-        wa_raw = keep.tile([P, PACK, H], F32)
-        nc.sync.dma_start(wa_raw[:], wa.rearrange("(p j) c -> p j c", j=PACK))
-        for j in range(PACK):
-            nc.sync.dma_start(x_sc[j:P:32, :].bitcast(I32), x_scales[0, j:16:PACK, :].bitcast(I32))
-        offs_sb = load_list(offs, "offs_sb")
-        x_w = keep.tile([P, T], I32, align_bytes=64)
-        nc.sync.dma_start(x_w[:], x_words[0].rearrange("p n j -> p (n j)").bitcast(I32))
-        two_sb = load_list(two, "two_sb")
-        n1_sb = load_list(n1, "n1_sb")
-        n2_sb = load_list(n2, "n2_sb")
-        n3_sb = load_list(n3, "n3_sb")
-        wb_raw = keep.tile([P, PACK, N], F32)
-        nc.sync.dma_start(wb_raw[:], wb.rearrange("(p j) c -> p j c", j=PACK))
-        n4_sb = load_list(n4, "n4_sb")
-        n5_sb = load_list(n5, "n5_sb")
-
         g_rows = keep.tile([P, P], F32)
         nc.gpsimd.memset(g_rows[:], 0.0)
-        for row, g in ((0, gt), (PACK, gi)):
-            nc.gpsimd.dma_start(
+
+        def load_factor(row, g):
+            nc.sync.dma_start(
                 g_rows[row : row + PACK, :].rearrange("t (q r) -> t q r", r=8),
                 g.rearrange("(q t r) o -> t q (r o)", t=PACK, r=8),
             )
+
+        offs_sb = load_list(offs, "offs_sb")
+        two_sb = load_list(two, "two_sb")
+        for j in range(PACK):
+            nc.sync.dma_start(x_sc[j:P:32, :].bitcast(I32), x_scales[0, j:16:PACK, :].bitcast(I32))
+        wa_raw = keep.tile([P, PACK, H], F32)
+        nc.sync.dma_start(wa_raw[:], wa.rearrange("(p j) c -> p j c", j=PACK))
+        x_w = keep.tile([P, T], I32, align_bytes=64)
+        nc.sync.dma_start(x_w[:], x_words[0].rearrange("p n j -> p (n j)").bitcast(I32))
+        load_factor(0, gt)
+        load_factor(PACK, gi)
+        n1_sb = load_list(n1, "n1_sb")
+        n2_sb = load_list(n2, "n2_sb")
+        n3_sb = load_list(n3, "n3_sb")
+        n4_sb = load_list(n4, "n4_sb")
+        n5_sb = load_list(n5, "n5_sb")
+        wb_raw = keep.tile([P, PACK, N], F32, tag="wb_raw", align_bytes=64)
+        nc.sync.dma_start(wb_raw[:], wb.rearrange("(p j) c -> p j c", j=PACK))
+
         ident = keep.tile([P, P], F32)
         make_identity(nc, ident[:])
+        ident_bf = keep.tile([P, P], BF16)
+        nc.scalar.copy(ident_bf[:], ident[:])
 
         a_win = [keep.tile([P, WIN], F32, name="a_win%d" % t) for t in range(PACK)]
         ex_win = [keep.tile([P, WIN], F32, name="ex_win%d" % t) for t in range(PACK)]
@@ -91,8 +97,8 @@ def tile_picked_momtop2lse_none_p_kernel(
             )
             return dealt
 
-        def pick_words(offsets, name):
-            dealt = keep.tile([P, S], U32, name=name, align_bytes=64)
+        def pick_words(offsets, name, tag):
+            dealt = keep.tile([P, S], U32, name=name, tag=tag, align_bytes=64)
             nc.vector.tensor_copy(
                 dealt[:].rearrange("p (t q r) -> p q t r", t=PACK, r=8),
                 x_w[:].bitcast(U32).indirect(offsets[:]),
@@ -125,14 +131,14 @@ def tile_picked_momtop2lse_none_p_kernel(
         wa_codes = keep.tile([P, H], U32, align_bytes=64)
         wa_scales = keep.tile([P, H], U8, align_bytes=64)
         half = H // 2
-        for h, copy in ((0, nc.vector.tensor_copy), (1, nc.scalar.copy)):
-            grouped = keep.tile([P, half * PACK], BF16, name="wa_grouped%d" % h, align_bytes=64)
+        for h, copy in ((0, nc.scalar.copy), (1, nc.scalar.copy)):
+            grouped = keep.tile([P, half * PACK], BF16, name="wa_grouped%d" % h, tag="wa_grouped%d" % h, align_bytes=64)
             cols = slice(h * half, (h + 1) * half)
             interleave(copy, grouped[:], wa_raw[:, :, cols])
             quantize(wa_codes[:, cols], wa_scales[:, cols], grouped[:])
 
-        xa_words = pick_words(offs_sb, "xa_words")
-        xb_words = pick_words(two_sb, "xb_words")
+        xa_words = pick_words(offs_sb, "xa_words", "wb_grouped")
+        xb_words = pick_words(two_sb, "xb_words", "wa_grouped1")
 
         for t in range(PACK):
             cols = slice(t * P, (t + 1) * P)
@@ -140,57 +146,120 @@ def tile_picked_momtop2lse_none_p_kernel(
             product(acc[:], xa_words[:, cols], xa_scales[:, cols], wa_codes[:], wa_scales[:])
             nc.scalar.activation(a_win[t][:, :H], acc[:], ACT.Copy, scale=gt_half[:, t : t + 1])
 
-        wb_grouped = keep.tile([P, N * PACK], BF16, align_bytes=64)
+        wb_grouped = keep.tile([P, N * PACK], BF16, tag="wb_grouped", align_bytes=64)
         interleave(nc.scalar.copy, wb_grouped[:], wb_raw[:])
         wb_codes = keep.tile([P, N], U32, align_bytes=64)
         wb_scales = keep.tile([P, N], U8, align_bytes=64)
 
         z_rows = keep.tile([P, PACK, H], BF16, align_bytes=64)
 
-        def top2_steps(t):
-            def tmp(name):
-                return work.tile([P, H], F32, name=name)
+        def fresh(name, tag):
+            return keep.tile([P, H], F32, name=name, tag=tag, align_bytes=64)[:]
 
-            b1, spread, hi, lead, bent = [tmp(name) for name in ("b1", "spread", "hi", "lead", "bent")]
-            d, e = ex_win[t][:, :H], ex_win[t][:, H:]
-            win = a_win[t]
+        early_spread = keep.tile([P, 2 * H], F32, tag="wb_raw", align_bytes=64)
+        spread = [early_spread[:, :H], early_spread[:, H:]]
+        b1 = [fresh("b1_%d" % t, "b1_%d" % t) for t in range(2)] * 2
+        d = [ex_win[t][:, :H] for t in range(PACK)]
+        e = {t: ex_win[t][:, H:] for t in range(3)}
+        lead = {3: ex_win[3][:, H:]}
+        hi = {t: fresh("hi%d" % t, "hi%d" % t) for t in (2, 3)}
 
-            def step_d():
-                nc.vector.tensor_tensor(d, win[:].indirect(n2_sb[:]), b1[:], ALU.subtract)
-                nc.scalar.activation(spread[:], d, ACT.Abs)
+        def step_b1(t):
+            nc.vector.tensor_copy(b1[t], a_win[t][:].indirect(n1_sb[:]))
 
-            return [
-                lambda: nc.vector.tensor_copy(b1[:], win[:].indirect(n1_sb[:])),
-                step_d,
-                lambda: nc.vector.scalar_tensor_tensor(hi[:], d, 0.0, b1[:], ALU.max, ALU.add),
-                lambda: nc.vector.tensor_tensor(e, win[:].indirect(n3_sb[:]), hi[:], ALU.subtract),
-                lambda: nc.vector.scalar_tensor_tensor(lead[:], e, -1.0, spread[:], ALU.mult, ALU.min),
-                lambda: nc.vector.scalar_tensor_tensor(bent[:], lead[:], -2.0, lead[:], ALU.mult, ALU.max),
-                lambda: nc.vector.tensor_tensor(z_rows[:, t, :], bent[:], hi[:], ALU.add),
-            ]
+        def step_d(t):
+            nc.vector.tensor_tensor(d[t], a_win[t][:].indirect(n2_sb[:]), b1[t], ALU.subtract)
 
-        def top2_pair(t):
-            for first, second in zip(top2_steps(t), top2_steps(t + 1)):
-                first()
-                second()
+        def step_spread(t):
+            nc.scalar.activation(spread[t], d[t], ACT.Abs)
 
-        top2_pair(0)
+        def step_hi(t):
+            nc.vector.scalar_tensor_tensor(hi[t], d[t], 0.0, b1[t], ALU.max, ALU.add)
+
+        def step_e(t):
+            nc.vector.tensor_tensor(e[t], a_win[t][:].indirect(n3_sb[:]), hi[t], ALU.subtract)
+
+        def step_lead(t):
+            nc.vector.scalar_tensor_tensor(lead[t], e[t], -1.0, spread[t], ALU.mult, ALU.min)
+
+        def sum_on_vector(t):
+            bent = work.tile([P, H], F32, name="bent")
+            nc.vector.scalar_tensor_tensor(bent[:], lead[t], -2.0, lead[t], ALU.mult, ALU.max)
+            nc.vector.tensor_tensor(z_rows[:, t, :], bent[:], hi[t], ALU.add)
+
+        excess = {}
+
+        def step_excess(t):
+            excess[t] = fresh("excess%d" % t, "z_turned0" if t == 2 else "excess%d" % t)
+            nc.scalar.activation(excess[t], e[t], ACT.Relu, scale=3.0)
+
+        def sum_on_tensor(t):
+            turned = bank(t)
+            terms = (excess[t], hi[t], lead[t])
+            for n, term in enumerate(terms):
+                for c in range(PACK):
+                    cols = slice(c * P, (c + 1) * P)
+                    nc.tensor.matmul(
+                        turned[:, cols], term[:, cols], ident[:],
+                        start=(n == 0 and c == 0), stop=(n == len(terms) - 1 and c == PACK - 1), is_transpose=True,
+                    )
+            z_turned = keep.tile([P, H], BF16, name="z_turned%d" % t, tag="z_turned%d" % t, align_bytes=64)
+            nc.scalar.copy(z_turned[:], turned[:])
+            back = bank(3, BF16)
+            for c in range(PACK):
+                cols = slice(c * P, (c + 1) * P)
+                nc.tensor.transpose(back[:, cols], z_turned[:, cols], ident_bf[:])
+            nc.scalar.copy(z_rows[:, t, :], back[:])
+
+        for step in (step_b1, step_d, step_spread):
+            step(0)
+            step(1)
 
         quantize(wb_codes[:], wb_scales[:], wb_grouped[:])
-        z2_rows = keep.tile([P, PACK, N], BF16, align_bytes=64)
+        early_hi = keep.tile([P, 2 * H], F32, tag="wb_grouped", align_bytes=64)
+        hi[0], hi[1] = early_hi[:, :H], early_hi[:, H:]
+        for step in (step_hi, step_e):
+            step(0)
+            step(1)
+        z2_rows = keep.tile([P, PACK, N], BF16, tag="z2_rows", align_bytes=64)
         for t in range(PACK):
             cols = slice(t * P, (t + 1) * P)
             acc = bank(PACK + t)
             product(acc[:], xb_words[:, cols], xb_scales[:, cols], wb_codes[:], wb_scales[:])
             nc.scalar.activation(z2_rows[:, t, :], acc[:], ACT.Copy, scale=gi_signed[:, t : t + 1])
-        z2_grouped = keep.tile([P, N * PACK], BF16, align_bytes=64)
+
+        for t in (0, 1):
+            lead[t] = fresh("lead%d" % t, "lead%d" % t)
+        step_excess(0)
+        step_excess(1)
+        step_lead(0)
+        sum_on_tensor(0)
+        step_b1(2)
+        step_lead(1)
+        sum_on_tensor(1)
+        step_d(2)
+        z2_grouped = keep.tile([P, N * PACK], BF16, tag="z2_grouped", align_bytes=64)
         interleave(nc.scalar.copy, z2_grouped[:], z2_rows[:])
-
-        top2_pair(2)
-
+        late_spread = keep.tile([P, 2 * H], F32, tag="z2_rows", align_bytes=64)
+        spread.extend([late_spread[:, :H], late_spread[:, H:]])
+        step_spread(2)
+        step_b1(3)
+        step_hi(2)
+        step_d(3)
+        step_spread(3)
+        step_e(2)
+        step_excess(2)
+        step_hi(3)
         z2_codes = keep.tile([P, N], U32, align_bytes=64)
         z2_scales = keep.tile([P, N], U8, align_bytes=64)
         quantize(z2_codes[:], z2_scales[:], z2_grouped[:])
+        lead[2] = fresh("lead2", "z2_grouped")
+        step_lead(2)
+        sum_on_tensor(2)
+        e[3] = spread[2]
+        step_e(3)
+        step_lead(3)
+        sum_on_vector(3)
 
         z_by_block = z_rows[:].rearrange("p t (g u c i) -> p u g c t i", g=8, u=PACK, i=4)
         z_grouped = [keep.tile([P, P * PACK], BF16, name="z_grouped%d" % u, align_bytes=64) for u in range(PACK)]
@@ -221,9 +290,17 @@ def tile_picked_momtop2lse_none_p_kernel(
             nc.vector.tensor_tensor(pair_sum[u][:], ex_win[u][:].indirect(n4_sb[:]), ex[u][:], ALU.add)
         out_rows = out.rearrange("(g u r) n -> u g r n", u=PACK, r=16)
         for u in range(PACK):
-            nc.scalar.activation(a_win[u][:, :N], cv_acc[u][:], ACT.Copy, scale=-0.0625)
+            if u == 0:
+                nc.vector.tensor_scalar_mul(a_win[u][:, :N], cv_acc[u][:], -0.0625)
+            else:
+                nc.scalar.activation(a_win[u][:, :N], cv_acc[u][:], ACT.Copy, scale=-0.0625)
             lse = work.tile([P, N], F32, name="lse")
             nc.scalar.activation(lse[:], pair_sum[u][:], ACT.Ln)
-            res = keep.tile([P, N], F32, name="res%d" % u)
-            nc.vector.tensor_tensor(res[:], a_win[u][:].indirect(n5_sb[:]), lse[:], ALU.add)
-            nc.sync.dma_start(out_rows[u], res[:])
+            pieces = 2 if u == PACK - 1 else 1
+            width = N // pieces
+            for h in range(pieces):
+                cols = slice(h * width, (h + 1) * width)
+                entries = n5_sb[:, h * width // 16 : (h + 1) * width // 16]
+                res = keep.tile([P, width], F32, name="res%d_%d" % (u, h))
+                nc.vector.tensor_tensor(res[:], a_win[u][:].indirect(entries), lse[:, cols], ALU.add)
+                nc.sync.dma_start(out_rows[u][:, :, cols], res[:])

@@ -182,10 +182,26 @@ def tile_picked_momtop2lse_none_p_kernel(
         def step_lead(t):
             nc.vector.scalar_tensor_tensor(lead[t], e[t], -1.0, spread[t], ALU.mult, ALU.min)
 
-        def sum_on_vector(t):
-            bent = work.tile([P, H], F32, name="bent")
-            nc.vector.scalar_tensor_tensor(bent[:], lead[t], -2.0, lead[t], ALU.mult, ALU.max)
-            nc.vector.tensor_tensor(z_rows[:, t, :], bent[:], hi[t], ALU.add)
+        def finish_on_vector(t):
+            for h in range(2):
+                cols = slice(h * half, (h + 1) * half)
+                entries = n3_sb[:, h * half // 16 : (h + 1) * half // 16]
+                nc.vector.tensor_tensor(e[t][:, cols], a_win[t][:].indirect(entries), hi[t][:, cols], ALU.subtract)
+            bent = fresh("bent", "bent")
+
+            def part(ap, h):
+                return ap.rearrange("p (g h r) -> p h g r", g=8, h=2)[:, h]
+
+            for h in range(2):
+                nc.vector.scalar_tensor_tensor(
+                    part(lead[t], h), part(e[t], h), -1.0, part(spread[t], h), ALU.mult, ALU.min
+                )
+            for h in range(2):
+                nc.vector.scalar_tensor_tensor(
+                    part(bent, h), part(lead[t], h), -2.0, part(lead[t], h), ALU.mult, ALU.max
+                )
+            for h in range(2):
+                nc.vector.tensor_tensor(part(z_rows[:, t, :], h), part(bent, h), part(hi[t], h), ALU.add)
 
         excess = {}
 
@@ -257,9 +273,7 @@ def tile_picked_momtop2lse_none_p_kernel(
         step_lead(2)
         sum_on_tensor(2)
         e[3] = spread[2]
-        step_e(3)
-        step_lead(3)
-        sum_on_vector(3)
+        finish_on_vector(3)
 
         z_by_block = z_rows[:].rearrange("p t (g u c i) -> p u g c t i", g=8, u=PACK, i=4)
         z_grouped = [keep.tile([P, P * PACK], BF16, name="z_grouped%d" % u, align_bytes=64) for u in range(PACK)]
@@ -267,35 +281,39 @@ def tile_picked_momtop2lse_none_p_kernel(
         z_scales = keep.tile([P, H], U8, align_bytes=64)
 
         def group_z(u):
-            nc.vector.tensor_copy(
+            copy = nc.scalar.copy if u == PACK - 1 else nc.vector.tensor_copy
+            copy(
                 z_grouped[u][:].rearrange("p (g c i t) -> p g c t i", g=8, i=4, t=PACK), z_by_block[:, u]
             )
 
         ex = [keep.tile([P, N], F32, name="ex%d" % u) for u in range(PACK)]
         cv_acc = []
+        group_z(PACK - 1)
         group_z(0)
         for u in range(PACK):
             cols = slice(u * P, (u + 1) * P)
-            if u + 1 < PACK:
+            if u + 2 < PACK:
                 group_z(u + 1)
             quantize(z_codes[:, cols], z_scales[:, cols], z_grouped[u][:])
             acc = bank(u)
             product(acc[:], z_codes[:, cols], z_scales[:, cols], z2_codes[:], z2_scales[:])
             nc.scalar.activation(ex_win[u][:, :N], acc[:], ACT.Exp, scale=0.0625)
-            nc.scalar.activation(ex[u][:], acc[:], ACT.Exp, scale=0.0625)
+            if u >= 2:
+                nc.scalar.activation(ex[u][:], acc[:], ACT.Exp, scale=0.0625)
             cv_acc.append(acc)
 
-        pair_sum = [keep.tile([P, N], F32, name="pair_sum%d" % u) for u in range(PACK)]
-        for u in range(PACK):
-            nc.vector.tensor_tensor(pair_sum[u][:], ex_win[u][:].indirect(n4_sb[:]), ex[u][:], ALU.add)
+        pair_sum = [a_win[u + 1][:, :N] for u in range(PACK - 1)] + [fresh("last_sum", "last_sum")]
+        for u in range(2):
+            nc.vector.tensor_copy(ex[u][:], ex_win[u][:].indirect(n4_sb[:]))
+        for u in range(2):
+            nc.vector.tensor_tensor(pair_sum[u], ex[u][:], ex_win[u][:, :N], ALU.add)
+        for u in range(2, PACK):
+            nc.vector.tensor_tensor(pair_sum[u], ex_win[u][:].indirect(n4_sb[:]), ex[u][:], ALU.add)
         out_rows = out.rearrange("(g u r) n -> u g r n", u=PACK, r=16)
         for u in range(PACK):
-            if u == 0:
-                nc.vector.tensor_scalar_mul(a_win[u][:, :N], cv_acc[u][:], -0.0625)
-            else:
-                nc.scalar.activation(a_win[u][:, :N], cv_acc[u][:], ACT.Copy, scale=-0.0625)
-            lse = work.tile([P, N], F32, name="lse")
-            nc.scalar.activation(lse[:], pair_sum[u][:], ACT.Ln)
+            nc.scalar.activation(a_win[u][:, :N], cv_acc[u][:], ACT.Copy, scale=-0.0625)
+            lse = keep.tile([P, N], F32, name="lse%d" % u)
+            nc.scalar.activation(lse[:], pair_sum[u], ACT.Ln)
             pieces = 2 if u == PACK - 1 else 1
             width = N // pieces
             for h in range(pieces):

from contextlib import ExitStack

import concourse.mybir as mybir
from concourse.masks import make_identity

K, T, S, H, N = 512, 2048, 512, 512, 512
P = 128
PACK = 4
WIN = 1024

F32 = mybir.dt.float32
BF16 = mybir.dt.bfloat16
I32 = mybir.dt.int32
U32 = mybir.dt.uint32
U16 = mybir.dt.uint16
U8 = mybir.dt.uint8
FP8X4 = mybir.dt.float8_e4m3fn_x4
ALU = mybir.AluOpType
ACT = mybir.ActivationFunctionType

FLOPS = 2 * K * S * H + 2 * K * S * N + 2 * S * H * N


def tile_picked_momtop2lse_none_p_kernel(
    tc, x_words, x_scales, wa, wb, gt, gi, offs, two, n1, n2, n3, n4, n5, out
):
    nc = tc.nc
    with ExitStack() as ctx:
        lists = ctx.enter_context(tc.tile_pool(name="lists", bufs=1))
        keep = ctx.enter_context(tc.tile_pool(name="keep", bufs=1))
        work = ctx.enter_context(tc.tile_pool(name="work", bufs=2))
        psum = ctx.enter_context(tc.psum_pool(name="psum", bufs=1))

        def load_list(src, name):
            tile = lists.tile([P, S // 16], U16, name=name)
            nc.sync.dma_start(tile[:], src)
            return tile

        def bank(b, dtype=F32):
            return psum.tile([P, 512], dtype, name="bank%d" % b)

        x_sc = keep.tile([P, T], U8, align_bytes=64)
        nc.vector.memset(x_sc[:].bitcast(I32), 0)
        g_rows = keep.tile([P, P], F32)
        nc.gpsimd.memset(g_rows[:], 0.0)

        def load_factor(row, g):
            nc.sync.dma_start(
                g_rows[row : row + PACK, :].rearrange("t (q r) -> t q r", r=8),
                g.rearrange("(q t r) o -> t q (r o)", t=PACK, r=8),
            )

        offs_sb = load_list(offs, "offs_sb")
        two_sb = load_list(two, "two_sb")
        for j in range(PACK):
            nc.sync.dma_start(x_sc[j:P:32, :].bitcast(I32), x_scales[0, j:16:PACK, :].bitcast(I32))
        wa_raw = keep.tile([P, PACK, H], F32)
        nc.sync.dma_start(wa_raw[:], wa.rearrange("(p j) c -> p j c", j=PACK))
        x_w = keep.tile([P, T], I32, align_bytes=64)
        nc.sync.dma_start(x_w[:], x_words[0].rearrange("p n j -> p (n j)").bitcast(I32))
        load_factor(0, gt)
        load_factor(PACK, gi)
        n1_sb = load_list(n1, "n1_sb")
        n2_sb = load_list(n2, "n2_sb")
        n3_sb = load_list(n3, "n3_sb")
        n4_sb = load_list(n4, "n4_sb")
        n5_sb = load_list(n5, "n5_sb")
        wb_raw = keep.tile([P, PACK, N], F32, tag="wb_raw", align_bytes=64)
        nc.sync.dma_start(wb_raw[:], wb.rearrange("(p j) c -> p j c", j=PACK))

        ident = keep.tile([P, P], F32)
        make_identity(nc, ident[:])
        ident_bf = keep.tile([P, P], BF16)
        nc.scalar.copy(ident_bf[:], ident[:])

        a_win = [keep.tile([P, WIN], F32, name="a_win%d" % t) for t in range(PACK)]
        ex_win = [keep.tile([P, WIN], F32, name="ex_win%d" % t) for t in range(PACK)]
        for t in range(PACK):
            nc.vector.memset(a_win[t][:, H:], 0.0)

        g_cols = bank(7)
        nc.tensor.transpose(g_cols[:, :P], g_rows[:], ident[:])
        gt_half = keep.tile([P, PACK], F32)
        nc.scalar.activation(gt_half[:], g_cols[:, 0:PACK], ACT.Abs, scale=0.5)
        gt_sign = keep.tile([P, PACK], F32)
        nc.scalar.activation(gt_sign[:], g_cols[:, 0:PACK], ACT.Sign)
        gi_signed = keep.tile([P, PACK], F32)
        nc.vector.tensor_tensor(gi_signed[:], g_cols[:, PACK : 2 * PACK], gt_sign[:], ALU.mult)

        def pick_scales(offsets, name):
            picked = keep.tile([P, S], U8, name=name + "_picked", align_bytes=64)
            nc.vector.tensor_copy(picked[:], x_sc[:].indirect(offsets[:]))
            dealt = keep.tile([P, S], U8, name=name, align_bytes=64)
            nc.vector.tensor_copy(
                dealt[:].bitcast(I32).rearrange("p (t q w) -> p q t w", t=PACK, w=2),
                picked[:].bitcast(I32).rearrange("p (q t w) -> p q t w", t=PACK, w=2),
            )
            return dealt

        def pick_words(offsets, name, tag):
            dealt = keep.tile([P, S], U32, name=name, tag=tag, align_bytes=64)
            nc.vector.tensor_copy(
                dealt[:].rearrange("p (t q r) -> p q t r", t=PACK, r=8),
                x_w[:].bitcast(U32).indirect(offsets[:]),
            )
            return dealt

        def interleave(copy, dst, src):
            copy(
                dst.rearrange("p (c i t) -> p c t i", i=4, t=PACK),
                src.rearrange("p t (c i) -> p c t i", i=4),
            )

        def quantize(codes, scales, grouped):
            nc.vector.quantize_mx(out=codes.bitcast(FP8X4), scales=scales, in_=grouped)

        def product(acc, lhs, lhs_scales, rhs, rhs_scales):
            nc.tensor.matmul_mx(
                out=acc,
                lhsT=lhs.bitcast(FP8X4),
                lhsT_scale=lhs_scales,
                rhs=rhs.bitcast(FP8X4),
                rhs_scale=rhs_scales,
                start=True,
                stop=True,
            )

        xa_scales = pick_scales(offs_sb, "xa_scales")
        xb_scales = pick_scales(two_sb, "xb_scales")

        wa_codes = keep.tile([P, H], U32, align_bytes=64)
        wa_scales = keep.tile([P, H], U8, align_bytes=64)
        half = H // 2
        for h, copy in ((0, nc.scalar.copy), (1, nc.scalar.copy)):
            grouped = keep.tile([P, half * PACK], BF16, name="wa_grouped%d" % h, tag="wa_grouped%d" % h, align_bytes=64)
            cols = slice(h * half, (h + 1) * half)
            interleave(copy, grouped[:], wa_raw[:, :, cols])
            quantize(wa_codes[:, cols], wa_scales[:, cols], grouped[:])

        xa_words = pick_words(offs_sb, "xa_words", "wb_grouped")
        xb_words = pick_words(two_sb, "xb_words", "wa_grouped1")

        for t in range(PACK):
            cols = slice(t * P, (t + 1) * P)
            acc = bank(t)
            product(acc[:], xa_words[:, cols], xa_scales[:, cols], wa_codes[:], wa_scales[:])
            nc.scalar.activation(a_win[t][:, :H], acc[:], ACT.Copy, scale=gt_half[:, t : t + 1])

        wb_grouped = keep.tile([P, N * PACK], BF16, tag="wb_grouped", align_bytes=64)
        interleave(nc.scalar.copy, wb_grouped[:], wb_raw[:])
        wb_codes = keep.tile([P, N], U32, align_bytes=64)
        wb_scales = keep.tile([P, N], U8, align_bytes=64)

        z_rows = keep.tile([P, PACK, H], BF16, align_bytes=64)

        def fresh(name, tag):
            return keep.tile([P, H], F32, name=name, tag=tag, align_bytes=64)[:]

        early_spread = keep.tile([P, 2 * H], F32, tag="wb_raw", align_bytes=64)
        spread = [early_spread[:, :H], early_spread[:, H:]]
        b1 = [fresh("b1_%d" % t, "b1_%d" % t) for t in range(2)] * 2
        d = [ex_win[t][:, :H] for t in range(PACK)]
        e = {t: ex_win[t][:, H:] for t in range(3)}
        lead = {3: ex_win[3][:, H:]}
        hi = {t: fresh("hi%d" % t, "hi%d" % t) for t in (2, 3)}

        def step_b1(t):
            nc.vector.tensor_copy(b1[t], a_win[t][:].indirect(n1_sb[:]))

        def step_d(t):
            nc.vector.tensor_tensor(d[t], a_win[t][:].indirect(n2_sb[:]), b1[t], ALU.subtract)

        def step_spread(t):
            nc.scalar.activation(spread[t], d[t], ACT.Abs)

        def step_hi(t):
            nc.vector.scalar_tensor_tensor(hi[t], d[t], 0.0, b1[t], ALU.max, ALU.add)

        def step_e(t):
            nc.vector.tensor_tensor(e[t], a_win[t][:].indirect(n3_sb[:]), hi[t], ALU.subtract)

        def step_lead(t):
            nc.vector.scalar_tensor_tensor(lead[t], e[t], -1.0, spread[t], ALU.mult, ALU.min)

        def finish_on_vector(t):
            for h in range(2):
                cols = slice(h * half, (h + 1) * half)
                entries = n3_sb[:, h * half // 16 : (h + 1) * half // 16]
                nc.vector.tensor_tensor(e[t][:, cols], a_win[t][:].indirect(entries), hi[t][:, cols], ALU.subtract)
            bent = fresh("bent", "bent")

            def part(ap, h):
                return ap.rearrange("p (g h r) -> p h g r", g=8, h=2)[:, h]

            for h in range(2):
                nc.vector.scalar_tensor_tensor(
                    part(lead[t], h), part(e[t], h), -1.0, part(spread[t], h), ALU.mult, ALU.min
                )
            for h in range(2):
                nc.vector.scalar_tensor_tensor(
                    part(bent, h), part(lead[t], h), -2.0, part(lead[t], h), ALU.mult, ALU.max
                )
            for h in range(2):
                nc.vector.tensor_tensor(part(z_rows[:, t, :], h), part(bent, h), part(hi[t], h), ALU.add)

        excess = {}

        def step_excess(t):
            excess[t] = fresh("excess%d" % t, "z_turned0" if t == 2 else "excess%d" % t)
            nc.scalar.activation(excess[t], e[t], ACT.Relu, scale=3.0)

        def sum_on_tensor(t):
            turned = bank(t)
            terms = (excess[t], hi[t], lead[t])
            for n, term in enumerate(terms):
                for c in range(PACK):
                    cols = slice(c * P, (c + 1) * P)
                    nc.tensor.matmul(
                        turned[:, cols], term[:, cols], ident[:],
                        start=(n == 0 and c == 0), stop=(n == len(terms) - 1 and c == PACK - 1), is_transpose=True,
                    )
            z_turned = keep.tile([P, H], BF16, name="z_turned%d" % t, tag="z_turned%d" % t, align_bytes=64)
            nc.scalar.copy(z_turned[:], turned[:])
            back = bank(3, BF16)
            for c in range(PACK):
                cols = slice(c * P, (c + 1) * P)
                nc.tensor.transpose(back[:, cols], z_turned[:, cols], ident_bf[:])
            nc.scalar.copy(z_rows[:, t, :], back[:])

        for step in (step_b1, step_d, step_spread):
            step(0)
            step(1)

        quantize(wb_codes[:], wb_scales[:], wb_grouped[:])
        early_hi = keep.tile([P, 2 * H], F32, tag="wb_grouped", align_bytes=64)
        hi[0], hi[1] = early_hi[:, :H], early_hi[:, H:]
        for step in (step_hi, step_e):
            step(0)
            step(1)
        z2_rows = keep.tile([P, PACK, N], BF16, tag="z2_rows", align_bytes=64)
        for t in range(PACK):
            cols = slice(t * P, (t + 1) * P)
            acc = bank(PACK + t)
            product(acc[:], xb_words[:, cols], xb_scales[:, cols], wb_codes[:], wb_scales[:])
            nc.scalar.activation(z2_rows[:, t, :], acc[:], ACT.Copy, scale=gi_signed[:, t : t + 1])

        for t in (0, 1):
            lead[t] = fresh("lead%d" % t, "lead%d" % t)
        step_excess(0)
        step_excess(1)
        step_lead(0)
        sum_on_tensor(0)
        step_b1(2)
        step_lead(1)
        sum_on_tensor(1)
        step_d(2)
        z2_grouped = keep.tile([P, N * PACK], BF16, tag="z2_grouped", align_bytes=64)
        interleave(nc.scalar.copy, z2_grouped[:], z2_rows[:])
        late_spread = keep.tile([P, 2 * H], F32, tag="z2_rows", align_bytes=64)
        spread.extend([late_spread[:, :H], late_spread[:, H:]])
        step_spread(2)
        step_b1(3)
        step_hi(2)
        step_d(3)
        step_spread(3)
        step_e(2)
        step_excess(2)
        step_hi(3)
        z2_codes = keep.tile([P, N], U32, align_bytes=64)
        z2_scales = keep.tile([P, N], U8, align_bytes=64)
        quantize(z2_codes[:], z2_scales[:], z2_grouped[:])
        lead[2] = fresh("lead2", "z2_grouped")
        step_lead(2)
        sum_on_tensor(2)
        e[3] = spread[2]
        finish_on_vector(3)

        z_by_block = z_rows[:].rearrange("p t (g u c i) -> p u g c t i", g=8, u=PACK, i=4)
        z_grouped = [keep.tile([P, P * PACK], BF16, name="z_grouped%d" % u, align_bytes=64) for u in range(PACK)]
        z_codes = keep.tile([P, H], U32, align_bytes=64)
        z_scales = keep.tile([P, H], U8, align_bytes=64)

        def group_z(u):
            copy = nc.scalar.copy if u == PACK - 1 else nc.vector.tensor_copy
            copy(
                z_grouped[u][:].rearrange("p (g c i t) -> p g c t i", g=8, i=4, t=PACK), z_by_block[:, u]
            )

        ex = [keep.tile([P, N], F32, name="ex%d" % u) for u in range(PACK)]
        cv_acc = []
        group_z(PACK - 1)
        group_z(0)
        for u in range(PACK):
            cols = slice(u * P, (u + 1) * P)
            if u + 2 < PACK:
                group_z(u + 1)
            quantize(z_codes[:, cols], z_scales[:, cols], z_grouped[u][:])
            acc = bank(u)
            product(acc[:], z_codes[:, cols], z_scales[:, cols], z2_codes[:], z2_scales[:])
            nc.scalar.activation(ex_win[u][:, :N], acc[:], ACT.Exp, scale=0.0625)
            if u >= 2:
                nc.scalar.activation(ex[u][:], acc[:], ACT.Exp, scale=0.0625)
            cv_acc.append(acc)

        pair_sum = [a_win[u + 1][:, :N] for u in range(PACK - 1)] + [fresh("last_sum", "last_sum")]
        for u in range(2):
            nc.vector.tensor_copy(ex[u][:], ex_win[u][:].indirect(n4_sb[:]))
        for u in range(2):
            nc.vector.tensor_tensor(pair_sum[u], ex[u][:], ex_win[u][:, :N], ALU.add)
        for u in range(2, PACK):
            nc.vector.tensor_tensor(pair_sum[u], ex_win[u][:].indirect(n4_sb[:]), ex[u][:], ALU.add)
        out_rows = out.rearrange("(g u r) n -> u g r n", u=PACK, r=16)
        for u in range(PACK):
            nc.scalar.activation(a_win[u][:, :N], cv_acc[u][:], ACT.Copy, scale=-0.0625)
            lse = keep.tile([P, N], F32, name="lse%d" % u)
            nc.scalar.activation(lse[:], pair_sum[u], ACT.Ln)
            pieces = 2 if u == PACK - 1 else 1
            width = N // pieces
            for h in range(pieces):
                cols = slice(h * width, (h + 1) * width)
                entries = n5_sb[:, h * width // 16 : (h + 1) * width // 16]
                res = keep.tile([P, width], F32, name="res%d_%d" % (u, h))
                nc.vector.tensor_tensor(res[:], a_win[u][:].indirect(entries), lse[:, cols], ALU.add)
                nc.sync.dma_start(out_rows[u][:, :, cols], res[:])
